import numpy as np
import ml_dtypes


def mxq(x, axis, fmt="e4m3"):
    dtype, down = {"e4m3": (ml_dtypes.float8_e4m3fn, 7), "e5m2": (ml_dtypes.float8_e5m2, 14)}[fmt]
    v = np.moveaxis(np.asarray(x, np.float32).astype(ml_dtypes.bfloat16).astype(np.float64), axis, -1)
    blocks = v.reshape(v.shape[:-1] + (-1, 32))
    amax = np.abs(blocks).max(-1, keepdims=True)
    byte = np.maximum(np.where(amax > 0, np.frexp(amax)[1] - 1 + 127, 0) - down, 1)
    scale = np.exp2(byte - 127.0)
    codes = (blocks / scale).astype(np.float32).astype(dtype).astype(np.float64)
    return np.moveaxis((codes * scale).reshape(v.shape), -1, axis)


WIDE = False


def mx_kscale(k):
    if not WIDE:
        return np.ones(k)
    levels = np.array([10, -10, 5, -5, 0])
    if k % 512:
        return np.exp2(np.random.permutation(np.resize(levels, k // 32))).repeat(32)
    a = np.empty((k // 512, 16))
    for p in range(k // 512):
        a[p, :8] = np.random.permutation(np.resize(levels, 8))
        for g in range(8):
            far = levels[np.abs(levels - a[p, g]) >= 10]
            a[p, g + 8] = far[np.random.randint(len(far))]
    return np.exp2(a.ravel()).repeat(32)


def f64(x):
    return np.asarray(x).astype(np.float64)


def striped(idx):
    return np.tile(idx.reshape(-1, 16).T, (8, 1)).astype(np.uint16)


def unstriped(offs):
    return offs[:16].T.reshape(-1).astype(np.int64)


E2M1 = np.array([0.0, 0.5, 1.0, 1.5, 2.0, 3.0, 4.0, 6.0, -0.0, -0.5, -1.0, -1.5, -2.0, -3.0, -4.0, -6.0])


def pack_weight(w, fmt):
    k, n = w.shape
    w = f64(np.asarray(w, np.float32).astype(ml_dtypes.bfloat16)).reshape(k // 32, 32, n)
    amax = np.abs(w).max(1)
    if fmt == "e4m3":
        byte = np.frexp(amax)[1] - 1 + 127 - 7
    else:
        mant, ex = np.frexp(amax / 6.0)
        byte = np.where(mant > 0.5, ex, ex - 1) + 127
    byte = np.clip(np.where(amax > 0, byte, 1), 1, 254)
    scaled = (w * np.exp2(127.0 - byte)[:, None, :]).reshape(k, n).astype(np.float32)
    by_word = np.ascontiguousarray(scaled.reshape(k // 512, 128, 4, n).transpose(0, 1, 3, 2))
    if fmt == "e4m3":
        words = by_word.astype(ml_dtypes.float8_e4m3fn).view(np.uint8)
    else:
        c = by_word.astype(ml_dtypes.float4_e2m1fn).view(np.uint8) & 0xF
        words = (c[..., 0::2] | (c[..., 1::2] << 4)).reshape(k // 512, 128, 2 * n)
    return np.ascontiguousarray(words), np.ascontiguousarray(byte.astype(np.uint8).reshape(k // 512, 16, n))


def unpack_weight(words, scales, fmt):
    g, _, n = scales.shape
    words = np.ascontiguousarray(words).reshape(g, 128, n, -1)
    if fmt == "e4m3":
        vals = words.view(ml_dtypes.float8_e4m3fn).astype(np.float64)
    else:
        nib = np.empty((g, 128, n, 4), np.uint8)
        nib[..., 0::2] = words & 0xF
        nib[..., 1::2] = words >> 4
        vals = E2M1[nib]
    vals = vals * np.repeat(np.exp2(scales.astype(np.float64) - 127.0), 8, axis=1)[..., None]
    return vals.transpose(0, 1, 3, 2).reshape(g * 512, n)


def gelu(v):
    return 0.5 * v * (1.0 + np.tanh(np.sqrt(2.0 / np.pi) * (v + 0.044715 * v**3)))


K, T, S, P, H, N = 1024, 4096, 1024, 512, 1536, 640


def setup_inputs():
    n = np.random.standard_normal
    s = mx_kscale(K)[:, None]
    u = mx_kscale(H)[:, None]
    d = {}
    d["tab_words"], d["tab_scales"] = pack_weight(n((K, T)) * s, "e2m1")
    d["offs"] = striped(np.random.permutation(T)[:S])
    d["pos1"] = striped(np.random.permutation(S)[:P])
    d["pos2"] = striped(np.random.permutation(S)[:P])
    d["w1"] = (1.3 * n((K, H)) / K ** 0.5 / s).astype(np.float32)
    d["b1"] = (0.5 * n(H)).astype(np.float32)
    d["gain"] = (np.random.uniform(0.6, 1.6, H) * u[:, 0]).astype(np.float32)
    d["w2_words"], d["w2_scales"] = pack_weight(n((H, N)) / H ** 0.5 / u, "e2m1")
    return d


def reference(tab_words, tab_scales, offs, pos1, pos2, w1, b1, gain, w2_words, w2_scales):
    v = unpack_weight(tab_words, tab_scales, "e2m1")[:, unstriped(offs)]
    e1 = mxq(f64(w1), 0, "e4m3").T @ v
    h = f64(gain)[:, None] * np.tanh(e1 + f64(b1)[:, None])
    tabs = h[:, unstriped(pos1)]
    sockets = h[:, unstriped(pos2)]
    both = mxq(tabs + sockets, 0, "e4m3")
    gap = mxq(np.abs(tabs - sockets), 0, "e4m3")
    w2 = unpack_weight(w2_words, w2_scales, "e2m1")
    y1 = w2.T @ both
    y2 = w2.T @ gap
    return np.minimum(y1, y2)

@@ -1,0 +1,250 @@
+from contextlib import ExitStack
+
+import concourse.mybir as mybir
+
+K, T, S, PAIRS, H, N = 1024, 4096, 1024, 512, 1536, 640
+FLOPS = 2 * K * H * S + 2 * 2 * H * N * PAIRS
+
+F32 = mybir.dt.float32
+BF16 = mybir.dt.bfloat16
+I32 = mybir.dt.int32
+U32 = mybir.dt.uint32
+U16 = mybir.dt.uint16
+U8 = mybir.dt.uint8
+FP8X4 = mybir.dt.float8_e4m3fn_x4
+FP4X4 = mybir.dt.float4_e2m1fn_x4
+ALU = mybir.AluOpType
+ACT = mybir.ActivationFunctionType
+
+P = 128
+PACK = 4
+K_PASS = P * PACK
+K_PASSES = K // K_PASS
+H_PASSES = H // K_PASS
+BANK = 512
+HALF = PAIRS // 2
+N_TILES = N // P
+FIRST_BANKS = (5, 6, 7)
+AHEAD = 2
+MP = 0
+CUTS = (0, 1, 3, 4, 6)
+
+
+def tile_list_jigsaw_edge_fit_kernel(
+    tc, tab_words, tab_scales, offs, pos1, pos2, w1, b1, gain, w2_words, w2_scales, out
+):
+    nc = tc.nc
+    with ExitStack() as ctx:
+        keep = ctx.enter_context(tc.tile_pool(name="keep", bufs=1))
+        ring = ctx.enter_context(tc.tile_pool(name="ring", bufs=2))
+        trio = ctx.enter_context(tc.tile_pool(name="trio", bufs=3))
+        rows = ctx.enter_context(tc.tile_pool(name="rows", bufs=8))
+        psum = ctx.enter_context(tc.psum_pool(name="psum", bufs=1))
+
+        offs_t = keep.tile([P, S // 16], U16)
+        pos1_t = keep.tile([P, PAIRS // 16], U16)
+        pos2_t = keep.tile([P, PAIRS // 16], U16)
+        table = [keep.tile([P, T], U16, name=f"table{a}", tag=f"table{a}", align_bytes=64) for a in range(K_PASSES)]
+        table_scales = keep.tile([P, T], U8, tag="scales", align_bytes=64)
+        v_words = [keep.tile([P, S], U16, name=f"v_words{a}", align_bytes=64) for a in range(K_PASSES)]
+        picked_scales = keep.tile([P, S], U8, align_bytes=64)
+        v_scales = [keep.tile([P, S], U8, name=f"v_scales{a}", align_bytes=64) for a in range(K_PASSES)]
+        bias_t = keep.tile([P, H_PASSES, PACK], F32)
+        gain_t = keep.tile([P, H_PASSES, PACK], F32)
+        gain2_t = keep.tile([P, H_PASSES, PACK], F32)
+
+        def load_w1(b, a):
+            raw = ring.tile([P, PACK, K_PASS], F32, name="raw", bufs=3)
+            src = w1[a * K_PASS : (a + 1) * K_PASS, b * K_PASS : (b + 1) * K_PASS]
+            nc.sync.dma_start(raw[:], src.rearrange("(p j) c -> p j c", j=PACK))
+            return raw
+
+        def quantise_w1(b, a, raw, casts):
+            grouped = ring.tile([P, PACK, P * PACK], BF16, name="grouped", align_bytes=64)
+            codes = keep.tile([P, K_PASS], U32, name=f"w1_codes{b}{a}", align_bytes=64)
+            scales = keep.tile([P, K_PASS], U8, name=f"w1_scales{b}{a}", align_bytes=64)
+            width = PACK // len(casts)
+            for part, cast in enumerate(casts):
+                ts = slice(part * width, (part + 1) * width)
+                cols = slice(part * width * P, (part + 1) * width * P)
+                cast(
+                    grouped[:, ts, :].rearrange("p t (m j) -> p m j t", j=PACK),
+                    raw[:].rearrange("p j (m t) -> p m j t", t=PACK)[:, :, :, ts],
+                )
+                nc.vector.quantize_mx(
+                    out=codes[:, cols].bitcast(FP8X4),
+                    scales=scales[:, cols],
+                    in_=grouped[:, ts, :].rearrange("p t c -> p (t c)"),
+                )
+            return codes, scales
+
+        def scalar_cast(dst, src):
+            nc.scalar.activation(dst, src, ACT.Copy)
+
+        nc.sync.dma_start(offs_t[:], offs)
+        for q in range(4):
+            nc.sync.dma_start(
+                table_scales[32 * q + 24 : 32 * q + 32, :].bitcast(I32),
+                tab_scales[:, 4 * q : 4 * q + 4, :].bitcast(I32),
+            )
+            engine = nc.vector if q % 2 == 0 else nc.gpsimd
+            engine.memset(table_scales[32 * q : 32 * q + 24, :].bitcast(I32), 0)
+        for a in range(K_PASSES):
+            nc.vector.memset(v_scales[a][:].bitcast(I32), 0)
+        nc.sync.dma_start(table[0][:].bitcast(I32), tab_words[0].bitcast(I32))
+        raw_first = load_w1(0, 0)
+        nc.sync.dma_start(table[1][:].bitcast(I32), tab_words[1].bitcast(I32))
+        raw_second = load_w1(0, 1)
+        nc.sync.dma_start(bias_t[:], b1.rearrange("(b p t) -> p b t", p=P, t=PACK))
+        nc.sync.dma_start(pos1_t[:], pos1)
+        nc.sync.dma_start(pos2_t[:], pos2)
+        nc.sync.dma_start(gain_t[:], gain.rearrange("(b p t) -> p b t", p=P, t=PACK))
+        nc.gpsimd.tensor_scalar(gain2_t[:], gain_t[:], 2.0, 0.0, ALU.mult, ALU.add)
+
+        nc.vector.tensor_copy(picked_scales[:], table_scales[:].indirect(offs_t[:]))
+        for a in range(K_PASSES):
+            shift = 24 + 4 * a
+            nc.scalar.dma_start(v_scales[a][0 : P - shift, :].bitcast(I32), picked_scales[shift:P, :].bitcast(I32))
+        w1q = {}
+        nc.vector.tensor_copy(v_words[0][:], table[0][:].indirect(offs_t[:]))
+        w1q[0, 0] = quantise_w1(0, 0, raw_first, [nc.vector.tensor_copy])
+        nc.vector.tensor_copy(v_words[1][:], table[1][:].indirect(offs_t[:]))
+        w1q[0, 1] = quantise_w1(0, 1, raw_second, [nc.vector.tensor_copy, scalar_cast])
+
+        w2_t = keep.tile([P, H_PASSES, 2 * N], U8, tag="table1", align_bytes=64)
+        w2_s = keep.tile([P, H_PASSES, N], U8, tag="scales", align_bytes=64)
+        nc.sync.dma_start(w2_t[:].bitcast(I32), w2_words.rearrange("a p c -> p a c").bitcast(I32))
+        nc.gpsimd.memset(w2_s[:].bitcast(I32), 0)
+        for q in range(4):
+            nc.sync.dma_start(
+                w2_s[32 * q : 32 * q + 4].bitcast(I32),
+                w2_scales[:, 4 * q : 4 * q + 4, :].rearrange("a r n -> r a n").bitcast(I32),
+            )
+
+        def first_stage(b, t):
+            h = rows.tile([P, S], F32, name="h", bufs=6)
+            cols = slice(t * P, (t + 1) * P)
+            for u in range(S // BANK):
+                turn = (b * PACK + t) * (S // BANK) + u
+                acc = psum.tile([P, BANK], F32, name="acc", tag=f"bank{FIRST_BANKS[turn % len(FIRST_BANKS)]}")
+                tok = slice(u * BANK, (u + 1) * BANK)
+                for a in range(K_PASSES):
+                    codes, scales = w1q[b, a]
+                    nc.tensor.matmul_mx(
+                        out=acc[:],
+                        lhsT=codes[:, cols].bitcast(FP8X4),
+                        lhsT_scale=scales[:, cols],
+                        rhs=v_words[a][:, tok].bitcast(FP4X4),
+                        rhs_scale=v_scales[a][:, tok],
+                        start=(a == 0),
+                        stop=(a == K_PASSES - 1),
+                    )
+                nc.scalar.activation(h[:, tok], acc[:], ACT.Tanh, bias=bias_t[:, b, t : t + 1])
+            return h
+
+        def pick(b, t, m0, m1):
+            h = hs[b, t]
+            both, gap = planes_of[b]
+            tabs = trio.tile([P, m1 - m0], F32, name="tabs")
+            cols = slice(m0, m1)
+            entries = slice(m0 // 16, m1 // 16)
+            nc.vector.tensor_copy(tabs[:], h[:].indirect(pos1_t[:, entries]))
+            nc.vector.tensor_tensor(both[:, t, cols], h[:].indirect(pos2_t[:, entries]), tabs[:], ALU.add)
+            nc.scalar.activation(both[:, t, cols], both[:, t, cols], ACT.Copy, scale=gain_t[:, b, t : t + 1])
+            nc.vector.scalar_tensor_tensor(
+                gap[:, t, cols], tabs[:], gain2_t[:, b, t : t + 1], both[:, t, cols], ALU.mult, ALU.subtract
+            )
+
+        def quantise_pairs(b, half):
+            both, gap = planes_of[b]
+            mixed = ring.tile([P, 2, HALF * PACK], BF16, name="mixed", align_bytes=64)
+            cols = slice(half * HALF, (half + 1) * HALF)
+            for kind, (planes, func) in enumerate(((both, ACT.Copy), (gap, ACT.Abs))):
+                nc.scalar.activation(
+                    mixed[:, kind, :].rearrange("p (c i t) -> p c t i", i=4, t=PACK),
+                    planes[:, :, cols].rearrange("p t (c i) -> p c t i", i=4),
+                    func,
+                )
+            codes = keep.tile([P, BANK], U32, name=f"pair_codes{b}{half}", align_bytes=64)
+            scales = keep.tile([P, BANK], U8, name=f"pair_scales{b}{half}", align_bytes=64)
+            nc.vector.quantize_mx(
+                out=codes[:].bitcast(FP8X4), scales=scales[:], in_=mixed[:].rearrange("p k c -> p (k c)")
+            )
+            pairq[b, half] = codes, scales
+
+        def second_stage(acc, b, half, nt):
+            codes, scales = pairq[b, half]
+            nc.tensor.matmul_mx(
+                out=acc[:],
+                lhsT=w2_t[:, b, 2 * P * nt : 2 * P * (nt + 1)].bitcast(FP4X4),
+                lhsT_scale=w2_s[:, b, P * nt : P * (nt + 1)],
+                rhs=codes[:].bitcast(FP8X4),
+                rhs_scale=scales[:],
+                start=(b == 0),
+                stop=(b == H_PASSES - 1),
+            )
+
+        def store(acc, half, nt):
+            y1 = rows.tile([P, HALF], F32, name="y1")
+            nc.scalar.copy(y1[:], acc[:, :HALF])
+            fit = rows.tile([P, HALF], F32, name="fit")
+            nc.vector.tensor_tensor(fit[:], acc[:, HALF:], y1[:], ALU.min)
+            nc.sync.dma_start(out[nt * P : (nt + 1) * P, half * HALF : (half + 1) * HALF], fit[:])
+
+        def sum_bank(bank):
+            return psum.tile([P, BANK], F32, name="sums", tag=f"bank{bank}")
+
+        hs = {}
+        pairq = {}
+        planes_of = {}
+        for b in range(H_PASSES):
+            planes_of[b] = (
+                keep.tile([P, PACK, PAIRS], F32, name=f"both{b}"),
+                keep.tile([P, PACK, PAIRS], F32, name=f"gap{b}"),
+            )
+        early = [sum_bank(nt) for nt in range(N_TILES)]
+        last = H_PASSES - 1
+        for t in range(AHEAD):
+            hs[0, t] = first_stage(0, t)
+        for t in range(PACK):
+            pick(0, t, 0, PAIRS)
+            b, a = divmod(K_PASSES + t, K_PASSES)
+            w1q[b, a] = quantise_w1(b, a, load_w1(b, a), [scalar_cast])
+            ahead = divmod(t + AHEAD, PACK)
+            hs[ahead] = first_stage(*ahead)
+        todo = [divmod(s, PACK) for s in range(PACK + AHEAD, H_PASSES * PACK)]
+        for t in range(PACK):
+            pick(1, t, 0, PAIRS)
+            if t % 2 == MP:
+                quantise_pairs(0, t // 2)
+            for ahead in todo[CUTS[t] : CUTS[t + 1]]:
+                hs[ahead] = first_stage(*ahead)
+        for nt in range(N_TILES):
+            second_stage(early[nt], 0, 0, nt)
+
+        late = [sum_bank(bank) for bank in FIRST_BANKS]
+        for nt in range(len(late)):
+            second_stage(late[nt], 0, 1, nt)
+        for t in range(PACK):
+            pick(last, t, 0, HALF)
+            if t % 2 == 0:
+                half = t // 2
+                quantise_pairs(last - 1, half)
+                sums = late if half else early
+                for nt in range(len(sums)):
+                    second_stage(sums[nt], last - 1, half, nt)
+        pick(last, 0, HALF, PAIRS)
+        quantise_pairs(last, 0)
+        for t in range(1, PACK):
+            pick(last, t, HALF, PAIRS)
+        for nt in range(N_TILES):
+            second_stage(early[nt], last, 0, nt)
+            store(early[nt], 0, nt)
+        for nt in range(len(FIRST_BANKS), N_TILES):
+            late.append(sum_bank(nt - len(FIRST_BANKS)))
+            for b in range(last):
+                second_stage(late[nt], b, 1, nt)
+        quantise_pairs(last, 1)
+        for nt in range(N_TILES):
+            second_stage(late[nt], last, 1, nt)
+            store(late[nt], 1, nt)

@@ -26,6 +26,7 @@ HALF = PAIRS // 2
 N_TILES = N // P
 FIRST_BANKS = (5, 6, 7)
 AHEAD = 2
+HT = 2
 MP = 0
 CUTS = (0, 1, 3, 4, 6)
 
@@ -44,7 +45,7 @@ def tile_list_jigsaw_edge_fit_kernel(
         offs_t = keep.tile([P, S // 16], U16)
         pos1_t = keep.tile([P, PAIRS // 16], U16)
         pos2_t = keep.tile([P, PAIRS // 16], U16)
-        table = [keep.tile([P, T], U16, name=f"table{a}", tag=f"table{a}", align_bytes=64) for a in range(K_PASSES)]
+        table = [keep.tile([P, T], U16, name=f"table{a}", tag=f"stage{2 * a}", align_bytes=64) for a in range(K_PASSES)]
         table_scales = keep.tile([P, T], U8, tag="scales", align_bytes=64)
         v_words = [keep.tile([P, S], U16, name=f"v_words{a}", align_bytes=64) for a in range(K_PASSES)]
         picked_scales = keep.tile([P, S], U8, align_bytes=64)
@@ -53,8 +54,8 @@ def tile_list_jigsaw_edge_fit_kernel(
         gain_t = keep.tile([P, H_PASSES, PACK], F32)
         gain2_t = keep.tile([P, H_PASSES, PACK], F32)
 
-        def load_w1(b, a):
-            raw = ring.tile([P, PACK, K_PASS], F32, name="raw", bufs=3)
+        def load_w1(b, a, stage):
+            raw = keep.tile([P, PACK, K_PASS], F32, name=f"raw{b}{a}", tag=f"stage{stage}", align_bytes=64)
             src = w1[a * K_PASS : (a + 1) * K_PASS, b * K_PASS : (b + 1) * K_PASS]
             nc.sync.dma_start(raw[:], src.rearrange("(p j) c -> p j c", j=PACK))
             return raw
@@ -68,8 +69,8 @@ def tile_list_jigsaw_edge_fit_kernel(
                 ts = slice(part * width, (part + 1) * width)
                 cols = slice(part * width * P, (part + 1) * width * P)
                 cast(
-                    grouped[:, ts, :].rearrange("p t (m j) -> p m j t", j=PACK),
-                    raw[:].rearrange("p j (m t) -> p m j t", t=PACK)[:, :, :, ts],
+                    grouped[:, ts, :].rearrange("p (u e) (m j) -> p u m j e", e=2, j=PACK),
+                    raw[:].rearrange("p j (m u e) -> p u m j e", u=2, e=2)[:, part * width // 2 : (part + 1) * width // 2],
                 )
                 nc.vector.quantize_mx(
                     out=codes[:, cols].bitcast(FP8X4),
@@ -77,9 +78,6 @@ def tile_list_jigsaw_edge_fit_kernel(
                     in_=grouped[:, ts, :].rearrange("p t c -> p (t c)"),
                 )
             return codes, scales
-
-        def scalar_cast(dst, src):
-            nc.scalar.activation(dst, src, ACT.Copy)
 
         nc.sync.dma_start(offs_t[:], offs)
         for q in range(4):
@@ -92,9 +90,9 @@ def tile_list_jigsaw_edge_fit_kernel(
         for a in range(K_PASSES):
             nc.vector.memset(v_scales[a][:].bitcast(I32), 0)
         nc.sync.dma_start(table[0][:].bitcast(I32), tab_words[0].bitcast(I32))
-        raw_first = load_w1(0, 0)
+        raw_first = load_w1(0, 0, 1)
         nc.sync.dma_start(table[1][:].bitcast(I32), tab_words[1].bitcast(I32))
-        raw_second = load_w1(0, 1)
+        raw_second = load_w1(0, 1, 3)
         nc.sync.dma_start(bias_t[:], b1.rearrange("(b p t) -> p b t", p=P, t=PACK))
         nc.sync.dma_start(pos1_t[:], pos1)
         nc.sync.dma_start(pos2_t[:], pos2)
@@ -109,20 +107,12 @@ def tile_list_jigsaw_edge_fit_kernel(
         nc.vector.tensor_copy(v_words[0][:], table[0][:].indirect(offs_t[:]))
         w1q[0, 0] = quantise_w1(0, 0, raw_first, [nc.vector.tensor_copy])
         nc.vector.tensor_copy(v_words[1][:], table[1][:].indirect(offs_t[:]))
-        w1q[0, 1] = quantise_w1(0, 1, raw_second, [nc.vector.tensor_copy, scalar_cast])
-
-        w2_t = keep.tile([P, H_PASSES, 2 * N], U8, tag="table1", align_bytes=64)
-        w2_s = keep.tile([P, H_PASSES, N], U8, tag="scales", align_bytes=64)
-        nc.sync.dma_start(w2_t[:].bitcast(I32), w2_words.rearrange("a p c -> p a c").bitcast(I32))
-        nc.gpsimd.memset(w2_s[:].bitcast(I32), 0)
-        for q in range(4):
-            nc.sync.dma_start(
-                w2_s[32 * q : 32 * q + 4].bitcast(I32),
-                w2_scales[:, 4 * q : 4 * q + 4, :].rearrange("a r n -> r a n").bitcast(I32),
-            )
+        w1q[0, 1] = quantise_w1(0, 1, raw_second, [nc.vector.tensor_copy, nc.scalar.copy])
 
         def first_stage(b, t):
-            h = rows.tile([P, S], F32, name="h", bufs=6)
+            s = b * PACK + t
+            tag = f"stage{s - AHEAD}" if AHEAD <= s < AHEAD + PACK else f"row{s}"
+            h = keep.tile([P, S], F32, name=f"h{s}", tag=tag, align_bytes=64)
             cols = slice(t * P, (t + 1) * P)
             for u in range(S // BANK):
                 turn = (b * PACK + t) * (S // BANK) + u
@@ -142,10 +132,11 @@ def tile_list_jigsaw_edge_fit_kernel(
                 nc.scalar.activation(h[:, tok], acc[:], ACT.Tanh, bias=bias_t[:, b, t : t + 1])
             return h
 
-        def pick(b, t, m0, m1):
+        def pick(b, t, m0, m1, tabs=None):
             h = hs[b, t]
             both, gap = planes_of[b]
-            tabs = trio.tile([P, m1 - m0], F32, name="tabs")
+            if tabs is None:
+                tabs = trio.tile([P, m1 - m0], F32, name="tabs")
             cols = slice(m0, m1)
             entries = slice(m0 // 16, m1 // 16)
             nc.vector.tensor_copy(tabs[:], h[:].indirect(pos1_t[:, entries]))
@@ -155,16 +146,18 @@ def tile_list_jigsaw_edge_fit_kernel(
                 gap[:, t, cols], tabs[:], gain2_t[:, b, t : t + 1], both[:, t, cols], ALU.mult, ALU.subtract
             )
 
-        def quantise_pairs(b, half):
+        def quantise_pairs(b, half, mixed=None, weave=None):
             both, gap = planes_of[b]
-            mixed = ring.tile([P, 2, HALF * PACK], BF16, name="mixed", align_bytes=64)
+            if mixed is None:
+                mixed = ring.tile([P, 2, HALF * PACK], BF16, name="mixed", align_bytes=64)
             cols = slice(half * HALF, (half + 1) * HALF)
             for kind, (planes, func) in enumerate(((both, ACT.Copy), (gap, ACT.Abs))):
-                nc.scalar.activation(
-                    mixed[:, kind, :].rearrange("p (c i t) -> p c t i", i=4, t=PACK),
-                    planes[:, :, cols].rearrange("p t (c i) -> p c t i", i=4),
-                    func,
-                )
+                dst = mixed[:, kind, :].rearrange("p (c i t) -> p c t i", i=2, t=PACK)
+                src = planes[:, :, cols].rearrange("p t (c i) -> p c t i", i=2)
+                if weave and kind == 0:
+                    weave(dst, src)
+                else:
+                    nc.scalar.activation(dst, src, func)
             codes = keep.tile([P, BANK], U32, name=f"pair_codes{b}{half}", align_bytes=64)
             scales = keep.tile([P, BANK], U8, name=f"pair_scales{b}{half}", align_bytes=64)
             nc.vector.quantize_mx(
@@ -209,9 +202,19 @@ def tile_list_jigsaw_edge_fit_kernel(
         for t in range(PACK):
             pick(0, t, 0, PAIRS)
             b, a = divmod(K_PASSES + t, K_PASSES)
-            w1q[b, a] = quantise_w1(b, a, load_w1(b, a), [scalar_cast])
+            w1q[b, a] = quantise_w1(b, a, load_w1(b, a, t), [nc.scalar.copy])
             ahead = divmod(t + AHEAD, PACK)
             hs[ahead] = first_stage(*ahead)
+        w2_t = keep.tile([P, H_PASSES, 2 * N], U8, tag="row0", align_bytes=64)
+        w2_s = keep.tile([P, H_PASSES, N], U8, tag="row1", align_bytes=64)
+        nc.sync.dma_start(w2_t[:].bitcast(I32), w2_words.rearrange("a p c -> p a c").bitcast(I32))
+        nc.gpsimd.memset(w2_s[:].bitcast(I32), 0)
+        for q in range(4):
+            nc.sync.dma_start(
+                w2_s[32 * q : 32 * q + 4].bitcast(I32),
+                w2_scales[:, 4 * q : 4 * q + 4, :].rearrange("a r n -> r a n").bitcast(I32),
+            )
+
         todo = [divmod(s, PACK) for s in range(PACK + AHEAD, H_PASSES * PACK)]
         for t in range(PACK):
             pick(1, t, 0, PAIRS)
@@ -233,18 +236,21 @@ def tile_list_jigsaw_edge_fit_kernel(
                 sums = late if half else early
                 for nt in range(len(sums)):
                     second_stage(sums[nt], last - 1, half, nt)
-        pick(last, 0, HALF, PAIRS)
-        quantise_pairs(last, 0)
-        for t in range(1, PACK):
-            pick(last, t, HALF, PAIRS)
+        held = keep.tile([P, 2, HALF * PACK], BF16, name="held", tag="held", align_bytes=64)
+        quantise_pairs(last, 0, held)
+        for t in range(PACK):
+            tabs = keep.tile([P, HALF], F32, name="after", tag="held", align_bytes=64) if t == HT else None
+            pick(last, t, HALF, PAIRS, tabs)
         for nt in range(N_TILES):
             second_stage(early[nt], last, 0, nt)
-            store(early[nt], 0, nt)
         for nt in range(len(FIRST_BANKS), N_TILES):
+            store(early[nt - len(FIRST_BANKS)], 0, nt - len(FIRST_BANKS))
             late.append(sum_bank(nt - len(FIRST_BANKS)))
             for b in range(last):
                 second_stage(late[nt], b, 1, nt)
-        quantise_pairs(last, 1)
+        quantise_pairs(last, 1, None, nc.vector.tensor_copy)
+        for nt in range(N_TILES - len(FIRST_BANKS), N_TILES):
+            store(early[nt], 0, nt)
         for nt in range(N_TILES):
             second_stage(late[nt], last, 1, nt)
             store(late[nt], 1, nt)

@@ -27,6 +27,8 @@ N_TILES = N // P
 FIRST_BANKS = (5, 6, 7)
 AHEAD = 2
 HT = 2
+REUSED = 3
+EARLY = 2
 MP = 0
 CUTS = (0, 1, 3, 4, 6)
 
@@ -85,8 +87,7 @@ def tile_list_jigsaw_edge_fit_kernel(
                 table_scales[32 * q + 24 : 32 * q + 32, :].bitcast(I32),
                 tab_scales[:, 4 * q : 4 * q + 4, :].bitcast(I32),
             )
-            engine = nc.vector if q % 2 == 0 else nc.gpsimd
-            engine.memset(table_scales[32 * q : 32 * q + 24, :].bitcast(I32), 0)
+            nc.vector.memset(table_scales[32 * q : 32 * q + 24, :].bitcast(I32), 0)
         for a in range(K_PASSES):
             nc.vector.memset(v_scales[a][:].bitcast(I32), 0)
         nc.sync.dma_start(table[0][:].bitcast(I32), tab_words[0].bitcast(I32))
@@ -140,8 +141,9 @@ def tile_list_jigsaw_edge_fit_kernel(
             cols = slice(m0, m1)
             entries = slice(m0 // 16, m1 // 16)
             nc.vector.tensor_copy(tabs[:], h[:].indirect(pos1_t[:, entries]))
-            nc.vector.tensor_tensor(both[:, t, cols], h[:].indirect(pos2_t[:, entries]), tabs[:], ALU.add)
-            nc.scalar.activation(both[:, t, cols], both[:, t, cols], ACT.Copy, scale=gain_t[:, b, t : t + 1])
+            sums = ring.tile([P, m1 - m0], F32, name="sums", bufs=2)
+            nc.vector.tensor_tensor(sums[:], h[:].indirect(pos2_t[:, entries]), tabs[:], ALU.add)
+            nc.scalar.activation(both[:, t, cols], sums[:], ACT.Copy, scale=gain_t[:, b, t : t + 1])
             nc.vector.scalar_tensor_tensor(
                 gap[:, t, cols], tabs[:], gain2_t[:, b, t : t + 1], both[:, t, cols], ALU.mult, ALU.subtract
             )
@@ -225,17 +227,16 @@ def tile_list_jigsaw_edge_fit_kernel(
         for nt in range(N_TILES):
             second_stage(early[nt], 0, 0, nt)
 
-        late = [sum_bank(bank) for bank in FIRST_BANKS]
-        for nt in range(len(late)):
-            second_stage(late[nt], 0, 1, nt)
+        late = {nt: sum_bank(FIRST_BANKS[nt - REUSED]) for nt in range(REUSED, N_TILES)}
         for t in range(PACK):
             pick(last, t, 0, HALF)
             if t % 2 == 0:
-                half = t // 2
-                quantise_pairs(last - 1, half)
-                sums = late if half else early
-                for nt in range(len(sums)):
-                    second_stage(sums[nt], last - 1, half, nt)
+                quantise_pairs(last - 1, t // 2)
+        for nt in range(N_TILES):
+            second_stage(early[nt], last - 1, 0, nt)
+        for nt in range(REUSED, N_TILES):
+            for b in range(last):
+                second_stage(late[nt], b, 1, nt)
         held = keep.tile([P, 2, HALF * PACK], BF16, name="held", tag="held", align_bytes=64)
         quantise_pairs(last, 0, held)
         for t in range(PACK):
@@ -243,14 +244,19 @@ def tile_list_jigsaw_edge_fit_kernel(
             pick(last, t, HALF, PAIRS, tabs)
         for nt in range(N_TILES):
             second_stage(early[nt], last, 0, nt)
-        for nt in range(len(FIRST_BANKS), N_TILES):
-            store(early[nt - len(FIRST_BANKS)], 0, nt - len(FIRST_BANKS))
-            late.append(sum_bank(nt - len(FIRST_BANKS)))
-            for b in range(last):
-                second_stage(late[nt], b, 1, nt)
-        quantise_pairs(last, 1, None, nc.vector.tensor_copy)
-        for nt in range(N_TILES - len(FIRST_BANKS), N_TILES):
+
+        def turn_over(nt):
             store(early[nt], 0, nt)
-        for nt in range(N_TILES):
+            if nt < REUSED:
+                late[nt] = sum_bank(nt)
+                for b in range(last):
+                    second_stage(late[nt], b, 1, nt)
+
+        for nt in range(EARLY):
+            turn_over(nt)
+        quantise_pairs(last, 1, None, nc.vector.tensor_copy)
+        for nt in range(EARLY, N_TILES):
+            turn_over(nt)
+        for nt in reversed(range(N_TILES)):
             second_stage(late[nt], last, 1, nt)
             store(late[nt], 1, nt)

@@ -26,6 +26,7 @@ HALF = PAIRS // 2
 N_TILES = N // P
 FIRST_BANKS = (5, 6, 7)
 AHEAD = 2
+SCALE_ROW0 = 96
 HT = 2
 REUSED = 3
 EARLY = 2
@@ -82,31 +83,32 @@ def tile_list_jigsaw_edge_fit_kernel(
             return codes, scales
 
         nc.sync.dma_start(offs_t[:], offs)
-        for q in range(4):
-            nc.sync.dma_start(
-                table_scales[32 * q + 24 : 32 * q + 32, :].bitcast(I32),
-                tab_scales[:, 4 * q : 4 * q + 4, :].bitcast(I32),
-            )
-            nc.vector.memset(table_scales[32 * q : 32 * q + 24, :].bitcast(I32), 0)
+        nc.sync.dma_start(
+            table_scales[SCALE_ROW0:P, :].bitcast(I32), tab_scales.rearrange("a q t -> (a q) t").bitcast(I32)
+        )
+        nc.vector.memset(table_scales[0:SCALE_ROW0, :].bitcast(I32), 0)
         for a in range(K_PASSES):
             nc.vector.memset(v_scales[a][:].bitcast(I32), 0)
+        nc.sync.dma_start(pos1_t[:], pos1)
+        nc.sync.dma_start(pos2_t[:], pos2)
         nc.sync.dma_start(table[0][:].bitcast(I32), tab_words[0].bitcast(I32))
         raw_first = load_w1(0, 0, 1)
         nc.sync.dma_start(table[1][:].bitcast(I32), tab_words[1].bitcast(I32))
         raw_second = load_w1(0, 1, 3)
-        nc.sync.dma_start(bias_t[:], b1.rearrange("(b p t) -> p b t", p=P, t=PACK))
-        nc.sync.dma_start(pos1_t[:], pos1)
-        nc.sync.dma_start(pos2_t[:], pos2)
-        nc.sync.dma_start(gain_t[:], gain.rearrange("(b p t) -> p b t", p=P, t=PACK))
+        nc.gpsimd.dma_start(bias_t[:], b1.rearrange("(b p t) -> p b t", p=P, t=PACK))
+        nc.gpsimd.dma_start(gain_t[:], gain.rearrange("(b p t) -> p b t", p=P, t=PACK))
         nc.gpsimd.tensor_scalar(gain2_t[:], gain_t[:], 2.0, 0.0, ALU.mult, ALU.add)
 
         nc.vector.tensor_copy(picked_scales[:], table_scales[:].indirect(offs_t[:]))
         for a in range(K_PASSES):
-            shift = 24 + 4 * a
-            nc.scalar.dma_start(v_scales[a][0 : P - shift, :].bitcast(I32), picked_scales[shift:P, :].bitcast(I32))
+            for q in range(4):
+                row = SCALE_ROW0 + 16 * a + 4 * q
+                nc.sync.dma_start(
+                    v_scales[a][32 * q : 32 * q + 4, :].bitcast(I32), picked_scales[row : row + 4, :].bitcast(I32)
+                )
         w1q = {}
         nc.vector.tensor_copy(v_words[0][:], table[0][:].indirect(offs_t[:]))
-        w1q[0, 0] = quantise_w1(0, 0, raw_first, [nc.vector.tensor_copy])
+        w1q[0, 0] = quantise_w1(0, 0, raw_first, [nc.vector.tensor_copy, nc.scalar.copy])
         nc.vector.tensor_copy(v_words[1][:], table[1][:].indirect(offs_t[:]))
         w1q[0, 1] = quantise_w1(0, 1, raw_second, [nc.vector.tensor_copy, nc.scalar.copy])
 
@@ -162,9 +164,14 @@ def tile_list_jigsaw_edge_fit_kernel(
                     nc.scalar.activation(dst, src, func)
             codes = keep.tile([P, BANK], U32, name=f"pair_codes{b}{half}", align_bytes=64)
             scales = keep.tile([P, BANK], U8, name=f"pair_scales{b}{half}", align_bytes=64)
-            nc.vector.quantize_mx(
-                out=codes[:].bitcast(FP8X4), scales=scales[:], in_=mixed[:].rearrange("p k c -> p (k c)")
-            )
+            if weave:
+                for kind in range(2):
+                    part = slice(kind * HALF, (kind + 1) * HALF)
+                    nc.vector.quantize_mx(out=codes[:, part].bitcast(FP8X4), scales=scales[:, part], in_=mixed[:, kind, :])
+            else:
+                nc.vector.quantize_mx(
+                    out=codes[:].bitcast(FP8X4), scales=scales[:], in_=mixed[:].rearrange("p k c -> p (k c)")
+                )
             pairq[b, half] = codes, scales
 
         def second_stage(acc, b, half, nt):

@@ -21,17 +21,18 @@ PACK = 4
 K_PASS = P * PACK
 K_PASSES = K // K_PASS
 H_PASSES = H // K_PASS
+LAST = H_PASSES - 1
+QUADRANTS = 4
 BANK = 512
 HALF = PAIRS // 2
 N_TILES = N // P
-FIRST_BANKS = (5, 6, 7)
+FIRST_STAGE_BANKS = (5, 6, 7)
+SCALE_ROW0 = P - 16 * K_PASSES
+SYNC_MOVES = 6
 AHEAD = 2
-SCALE_ROW0 = 96
-HT = 2
-REUSED = 3
-EARLY = 2
-MP = 0
-CUTS = (0, 1, 3, 4, 6)
+HELD_SLICE = 2
+REUSED_BANKS = 3
+EMPTIED_EARLY = 2
 
 
 def tile_list_jigsaw_edge_fit_kernel(
@@ -41,21 +42,25 @@ def tile_list_jigsaw_edge_fit_kernel(
     with ExitStack() as ctx:
         keep = ctx.enter_context(tc.tile_pool(name="keep", bufs=1))
         ring = ctx.enter_context(tc.tile_pool(name="ring", bufs=2))
-        trio = ctx.enter_context(tc.tile_pool(name="trio", bufs=3))
-        rows = ctx.enter_context(tc.tile_pool(name="rows", bufs=8))
+        tab_ring = ctx.enter_context(tc.tile_pool(name="tab_ring", bufs=3))
+        result_ring = ctx.enter_context(tc.tile_pool(name="result_ring", bufs=8))
         psum = ctx.enter_context(tc.psum_pool(name="psum", bufs=1))
 
         offs_t = keep.tile([P, S // 16], U16)
         pos1_t = keep.tile([P, PAIRS // 16], U16)
         pos2_t = keep.tile([P, PAIRS // 16], U16)
         table = [keep.tile([P, T], U16, name=f"table{a}", tag=f"stage{2 * a}", align_bytes=64) for a in range(K_PASSES)]
-        table_scales = keep.tile([P, T], U8, tag="scales", align_bytes=64)
+        table_scales = keep.tile([P, T], U8, align_bytes=64)
         v_words = [keep.tile([P, S], U16, name=f"v_words{a}", align_bytes=64) for a in range(K_PASSES)]
-        picked_scales = keep.tile([P, S], U8, align_bytes=64)
+        picked_scales = keep.tile([P, S], U8, tag="picked", align_bytes=64)
         v_scales = [keep.tile([P, S], U8, name=f"v_scales{a}", align_bytes=64) for a in range(K_PASSES)]
         bias_t = keep.tile([P, H_PASSES, PACK], F32)
         gain_t = keep.tile([P, H_PASSES, PACK], F32)
-        gain2_t = keep.tile([P, H_PASSES, PACK], F32)
+
+        w1_mx = {}
+        h_slices = {}
+        planes = {}
+        pair_mx = {}
 
         def load_w1(b, a, stage):
             raw = keep.tile([P, PACK, K_PASS], F32, name=f"raw{b}{a}", tag=f"stage{stage}", align_bytes=64)
@@ -63,24 +68,127 @@ def tile_list_jigsaw_edge_fit_kernel(
             nc.sync.dma_start(raw[:], src.rearrange("(p j) c -> p j c", j=PACK))
             return raw
 
-        def quantise_w1(b, a, raw, casts):
-            grouped = ring.tile([P, PACK, P * PACK], BF16, name="grouped", align_bytes=64)
+        def quantise_w1(b, a, raw, casts, grouped):
             codes = keep.tile([P, K_PASS], U32, name=f"w1_codes{b}{a}", align_bytes=64)
             scales = keep.tile([P, K_PASS], U8, name=f"w1_scales{b}{a}", align_bytes=64)
-            width = PACK // len(casts)
+            share = PACK // len(casts)
             for part, cast in enumerate(casts):
-                ts = slice(part * width, (part + 1) * width)
-                cols = slice(part * width * P, (part + 1) * width * P)
+                ts = slice(part * share, (part + 1) * share)
+                us = slice(ts.start // 2, ts.stop // 2)
+                cols = slice(ts.start * P, ts.stop * P)
                 cast(
                     grouped[:, ts, :].rearrange("p (u e) (m j) -> p u m j e", e=2, j=PACK),
-                    raw[:].rearrange("p j (m u e) -> p u m j e", u=2, e=2)[:, part * width // 2 : (part + 1) * width // 2],
+                    raw[:].rearrange("p j (m u e) -> p u m j e", u=2, e=2)[:, us],
                 )
                 nc.vector.quantize_mx(
                     out=codes[:, cols].bitcast(FP8X4),
                     scales=scales[:, cols],
                     in_=grouped[:, ts, :].rearrange("p t c -> p (t c)"),
                 )
+            w1_mx[b, a] = codes, scales
+
+        def grouped_tile():
+            return ring.tile([P, PACK, P * PACK], BF16, name="grouped", align_bytes=64)
+
+        def first_stage(b, t):
+            s = b * PACK + t
+            tag = f"stage{s - 1}" if AHEAD <= s <= PACK else f"row{s}"
+            h = keep.tile([P, S], F32, name=f"h{s}", tag=tag, align_bytes=64)
+            cols = slice(t * P, (t + 1) * P)
+            for u in range(S // BANK):
+                turn = s * (S // BANK) + u
+                bank = FIRST_STAGE_BANKS[turn % len(FIRST_STAGE_BANKS)]
+                acc = psum.tile([P, BANK], F32, name="acc", tag=f"bank{bank}")
+                picked = slice(u * BANK, (u + 1) * BANK)
+                for a in range(K_PASSES):
+                    codes, scales = w1_mx[b, a]
+                    nc.tensor.matmul_mx(
+                        out=acc[:],
+                        lhsT=codes[:, cols].bitcast(FP8X4),
+                        lhsT_scale=scales[:, cols],
+                        rhs=v_words[a][:, picked].bitcast(FP4X4),
+                        rhs_scale=v_scales[a][:, picked],
+                        start=(a == 0),
+                        stop=(a == K_PASSES - 1),
+                    )
+                nc.scalar.activation(h[:, picked], acc[:], ACT.Tanh, bias=bias_t[:, b, t : t + 1])
+            h_slices[b, t] = h
+
+        def tab_tile(width):
+            return tab_ring.tile([P, width], F32, name="tabs")
+
+        def pick(b, t, m0, m1, tabs):
+            h = h_slices[b, t]
+            both, gap = planes[b]
+            cols = slice(m0, m1)
+            entries = slice(m0 // 16, m1 // 16)
+            nc.vector.tensor_copy(tabs[:], h[:].indirect(pos1_t[:, entries]))
+            pair_sum = ring.tile([P, m1 - m0], F32, name="pair_sum")
+            nc.vector.tensor_tensor(pair_sum[:], h[:].indirect(pos2_t[:, entries]), tabs[:], ALU.add)
+            nc.scalar.activation(both[:, t, cols], pair_sum[:], ACT.Copy, scale=gain_t[:, b, t : t + 1])
+            nc.vector.scalar_tensor_tensor(
+                gap[:, t, cols], tabs[:], gain2_t[:, b, t : t + 1], both[:, t, cols], ALU.mult, ALU.subtract
+            )
+
+        def woven_views(b, half, woven):
+            cols = slice(half * HALF, (half + 1) * HALF)
+            return [
+                (
+                    woven[:, kind, :].rearrange("p (c i t) -> p c t i", i=2, t=PACK),
+                    plane[:, :, cols].rearrange("p t (c i) -> p c t i", i=2),
+                )
+                for kind, plane in enumerate(planes[b])
+            ]
+
+        def pair_tiles(b, half):
+            codes = keep.tile([P, BANK], U32, name=f"pair_codes{b}{half}", align_bytes=64)
+            scales = keep.tile([P, BANK], U8, name=f"pair_scales{b}{half}", align_bytes=64)
+            pair_mx[b, half] = codes, scales
             return codes, scales
+
+        def woven_tile():
+            return ring.tile([P, 2, HALF * PACK], BF16, name="woven", align_bytes=64)
+
+        def quantise_pairs(b, half, woven):
+            (both_dst, both_src), (gap_dst, gap_src) = woven_views(b, half, woven)
+            nc.scalar.activation(both_dst, both_src, ACT.Copy)
+            nc.scalar.activation(gap_dst, gap_src, ACT.Abs)
+            codes, scales = pair_tiles(b, half)
+            nc.vector.quantize_mx(
+                out=codes[:].bitcast(FP8X4), scales=scales[:], in_=woven[:].rearrange("p k c -> p (k c)")
+            )
+
+        def quantise_last_pairs():
+            woven = woven_tile()
+            (both_dst, both_src), (gap_dst, gap_src) = woven_views(LAST, 1, woven)
+            nc.vector.tensor_copy(both_dst, both_src)
+            nc.scalar.activation(gap_dst, gap_src, ACT.Abs)
+            codes, scales = pair_tiles(LAST, 1)
+            for kind in range(2):
+                part = slice(kind * HALF, (kind + 1) * HALF)
+                nc.vector.quantize_mx(out=codes[:, part].bitcast(FP8X4), scales=scales[:, part], in_=woven[:, kind, :])
+
+        def sum_bank(bank):
+            return psum.tile([P, BANK], F32, name="y", tag=f"bank{bank}")
+
+        def second_stage(y, b, half, nt):
+            codes, scales = pair_mx[b, half]
+            nc.tensor.matmul_mx(
+                out=y[:],
+                lhsT=w2_t[:, b, 2 * P * nt : 2 * P * (nt + 1)].bitcast(FP4X4),
+                lhsT_scale=w2_s[:, b, P * nt : P * (nt + 1)],
+                rhs=codes[:].bitcast(FP8X4),
+                rhs_scale=scales[:],
+                start=(b == 0),
+                stop=(b == LAST),
+            )
+
+        def store(y, half, nt):
+            y1 = result_ring.tile([P, HALF], F32, name="y1")
+            nc.scalar.copy(y1[:], y[:, :HALF])
+            fit = result_ring.tile([P, HALF], F32, name="fit")
+            nc.vector.tensor_tensor(fit[:], y[:, HALF:], y1[:], ALU.min)
+            nc.sync.dma_start(out[nt * P : (nt + 1) * P, half * HALF : (half + 1) * HALF], fit[:])
 
         nc.sync.dma_start(offs_t[:], offs)
         nc.sync.dma_start(
@@ -97,173 +205,101 @@ def tile_list_jigsaw_edge_fit_kernel(
         raw_second = load_w1(0, 1, 3)
         nc.gpsimd.dma_start(bias_t[:], b1.rearrange("(b p t) -> p b t", p=P, t=PACK))
         nc.gpsimd.dma_start(gain_t[:], gain.rearrange("(b p t) -> p b t", p=P, t=PACK))
-        nc.gpsimd.tensor_scalar(gain2_t[:], gain_t[:], 2.0, 0.0, ALU.mult, ALU.add)
 
         nc.vector.tensor_copy(picked_scales[:], table_scales[:].indirect(offs_t[:]))
         for a in range(K_PASSES):
-            for q in range(4):
+            for q in range(QUADRANTS):
                 row = SCALE_ROW0 + 16 * a + 4 * q
-                nc.sync.dma_start(
+                queue = nc.sync if QUADRANTS * a + q < SYNC_MOVES else nc.gpsimd
+                queue.dma_start(
                     v_scales[a][32 * q : 32 * q + 4, :].bitcast(I32), picked_scales[row : row + 4, :].bitcast(I32)
                 )
-        w1q = {}
+        gain2_t = keep.tile([P, H_PASSES, PACK], F32, tag="picked", align_bytes=64)
+        nc.gpsimd.tensor_scalar(gain2_t[:], gain_t[:], 2.0, 0.0, ALU.mult, ALU.add)
+        shared_cast = [nc.vector.tensor_copy, nc.scalar.copy]
         nc.vector.tensor_copy(v_words[0][:], table[0][:].indirect(offs_t[:]))
-        w1q[0, 0] = quantise_w1(0, 0, raw_first, [nc.vector.tensor_copy, nc.scalar.copy])
+        quantise_w1(0, 0, raw_first, shared_cast, grouped_tile())
         nc.vector.tensor_copy(v_words[1][:], table[1][:].indirect(offs_t[:]))
-        w1q[0, 1] = quantise_w1(0, 1, raw_second, [nc.vector.tensor_copy, nc.scalar.copy])
+        quantise_w1(0, 1, raw_second, shared_cast, grouped_tile())
 
-        def first_stage(b, t):
-            s = b * PACK + t
-            tag = f"stage{s - AHEAD}" if AHEAD <= s < AHEAD + PACK else f"row{s}"
-            h = keep.tile([P, S], F32, name=f"h{s}", tag=tag, align_bytes=64)
-            cols = slice(t * P, (t + 1) * P)
-            for u in range(S // BANK):
-                turn = (b * PACK + t) * (S // BANK) + u
-                acc = psum.tile([P, BANK], F32, name="acc", tag=f"bank{FIRST_BANKS[turn % len(FIRST_BANKS)]}")
-                tok = slice(u * BANK, (u + 1) * BANK)
-                for a in range(K_PASSES):
-                    codes, scales = w1q[b, a]
-                    nc.tensor.matmul_mx(
-                        out=acc[:],
-                        lhsT=codes[:, cols].bitcast(FP8X4),
-                        lhsT_scale=scales[:, cols],
-                        rhs=v_words[a][:, tok].bitcast(FP4X4),
-                        rhs_scale=v_scales[a][:, tok],
-                        start=(a == 0),
-                        stop=(a == K_PASSES - 1),
-                    )
-                nc.scalar.activation(h[:, tok], acc[:], ACT.Tanh, bias=bias_t[:, b, t : t + 1])
-            return h
-
-        def pick(b, t, m0, m1, tabs=None):
-            h = hs[b, t]
-            both, gap = planes_of[b]
-            if tabs is None:
-                tabs = trio.tile([P, m1 - m0], F32, name="tabs")
-            cols = slice(m0, m1)
-            entries = slice(m0 // 16, m1 // 16)
-            nc.vector.tensor_copy(tabs[:], h[:].indirect(pos1_t[:, entries]))
-            sums = ring.tile([P, m1 - m0], F32, name="sums", bufs=2)
-            nc.vector.tensor_tensor(sums[:], h[:].indirect(pos2_t[:, entries]), tabs[:], ALU.add)
-            nc.scalar.activation(both[:, t, cols], sums[:], ACT.Copy, scale=gain_t[:, b, t : t + 1])
-            nc.vector.scalar_tensor_tensor(
-                gap[:, t, cols], tabs[:], gain2_t[:, b, t : t + 1], both[:, t, cols], ALU.mult, ALU.subtract
-            )
-
-        def quantise_pairs(b, half, mixed=None, weave=None):
-            both, gap = planes_of[b]
-            if mixed is None:
-                mixed = ring.tile([P, 2, HALF * PACK], BF16, name="mixed", align_bytes=64)
-            cols = slice(half * HALF, (half + 1) * HALF)
-            for kind, (planes, func) in enumerate(((both, ACT.Copy), (gap, ACT.Abs))):
-                dst = mixed[:, kind, :].rearrange("p (c i t) -> p c t i", i=2, t=PACK)
-                src = planes[:, :, cols].rearrange("p t (c i) -> p c t i", i=2)
-                if weave and kind == 0:
-                    weave(dst, src)
-                else:
-                    nc.scalar.activation(dst, src, func)
-            codes = keep.tile([P, BANK], U32, name=f"pair_codes{b}{half}", align_bytes=64)
-            scales = keep.tile([P, BANK], U8, name=f"pair_scales{b}{half}", align_bytes=64)
-            if weave:
-                for kind in range(2):
-                    part = slice(kind * HALF, (kind + 1) * HALF)
-                    nc.vector.quantize_mx(out=codes[:, part].bitcast(FP8X4), scales=scales[:, part], in_=mixed[:, kind, :])
-            else:
-                nc.vector.quantize_mx(
-                    out=codes[:].bitcast(FP8X4), scales=scales[:], in_=mixed[:].rearrange("p k c -> p (k c)")
-                )
-            pairq[b, half] = codes, scales
-
-        def second_stage(acc, b, half, nt):
-            codes, scales = pairq[b, half]
-            nc.tensor.matmul_mx(
-                out=acc[:],
-                lhsT=w2_t[:, b, 2 * P * nt : 2 * P * (nt + 1)].bitcast(FP4X4),
-                lhsT_scale=w2_s[:, b, P * nt : P * (nt + 1)],
-                rhs=codes[:].bitcast(FP8X4),
-                rhs_scale=scales[:],
-                start=(b == 0),
-                stop=(b == H_PASSES - 1),
-            )
-
-        def store(acc, half, nt):
-            y1 = rows.tile([P, HALF], F32, name="y1")
-            nc.scalar.copy(y1[:], acc[:, :HALF])
-            fit = rows.tile([P, HALF], F32, name="fit")
-            nc.vector.tensor_tensor(fit[:], acc[:, HALF:], y1[:], ALU.min)
-            nc.sync.dma_start(out[nt * P : (nt + 1) * P, half * HALF : (half + 1) * HALF], fit[:])
-
-        def sum_bank(bank):
-            return psum.tile([P, BANK], F32, name="sums", tag=f"bank{bank}")
-
-        hs = {}
-        pairq = {}
-        planes_of = {}
         for b in range(H_PASSES):
-            planes_of[b] = (
+            planes[b] = (
                 keep.tile([P, PACK, PAIRS], F32, name=f"both{b}"),
                 keep.tile([P, PACK, PAIRS], F32, name=f"gap{b}"),
             )
-        early = [sum_bank(nt) for nt in range(N_TILES)]
-        last = H_PASSES - 1
+        first_half = [sum_bank(nt) for nt in range(N_TILES)]
         for t in range(AHEAD):
-            hs[0, t] = first_stage(0, t)
+            first_stage(0, t)
+
+        early_grouped = keep.tile([P, PACK, P * PACK], BF16, tag="early", align_bytes=64)
+        quantise_w1(1, 0, load_w1(1, 0, 0), [nc.vector.tensor_copy], early_grouped)
+        taken_over = ("stage0", "early")
         for t in range(PACK):
-            pick(0, t, 0, PAIRS)
-            b, a = divmod(K_PASSES + t, K_PASSES)
-            w1q[b, a] = quantise_w1(b, a, load_w1(b, a, t), [nc.scalar.copy])
-            ahead = divmod(t + AHEAD, PACK)
-            hs[ahead] = first_stage(*ahead)
+            if t < len(taken_over):
+                tabs = keep.tile([P, PAIRS], F32, name="first_tabs", tag=taken_over[t], align_bytes=64)
+            else:
+                tabs = tab_tile(PAIRS)
+            pick(0, t, 0, PAIRS, tabs)
+            if t + 1 < PACK:
+                b, a = divmod(K_PASSES + t + 1, K_PASSES)
+                quantise_w1(b, a, load_w1(b, a, t + 1), [nc.scalar.copy], grouped_tile())
+            first_stage(*divmod(t + AHEAD, PACK))
+
         w2_t = keep.tile([P, H_PASSES, 2 * N], U8, tag="row0", align_bytes=64)
         w2_s = keep.tile([P, H_PASSES, N], U8, tag="row1", align_bytes=64)
         nc.sync.dma_start(w2_t[:].bitcast(I32), w2_words.rearrange("a p c -> p a c").bitcast(I32))
         nc.gpsimd.memset(w2_s[:].bitcast(I32), 0)
-        for q in range(4):
+        for q in range(QUADRANTS):
             nc.sync.dma_start(
                 w2_s[32 * q : 32 * q + 4].bitcast(I32),
                 w2_scales[:, 4 * q : 4 * q + 4, :].rearrange("a r n -> r a n").bitcast(I32),
             )
 
-        todo = [divmod(s, PACK) for s in range(PACK + AHEAD, H_PASSES * PACK)]
+        next_slice = PACK + AHEAD
         for t in range(PACK):
-            pick(1, t, 0, PAIRS)
-            if t % 2 == MP:
-                quantise_pairs(0, t // 2)
-            for ahead in todo[CUTS[t] : CUTS[t + 1]]:
-                hs[ahead] = first_stage(*ahead)
-        for nt in range(N_TILES):
-            second_stage(early[nt], 0, 0, nt)
-
-        late = {nt: sum_bank(FIRST_BANKS[nt - REUSED]) for nt in range(REUSED, N_TILES)}
-        for t in range(PACK):
-            pick(last, t, 0, HALF)
+            pick(1, t, 0, PAIRS, tab_tile(PAIRS))
             if t % 2 == 0:
-                quantise_pairs(last - 1, t // 2)
+                quantise_pairs(0, t // 2, woven_tile())
+            made = 1 if t % 2 == 0 else 2
+            for s in range(next_slice, next_slice + made):
+                first_stage(*divmod(s, PACK))
+            next_slice = next_slice + made
         for nt in range(N_TILES):
-            second_stage(early[nt], last - 1, 0, nt)
-        for nt in range(REUSED, N_TILES):
-            for b in range(last):
-                second_stage(late[nt], b, 1, nt)
-        held = keep.tile([P, 2, HALF * PACK], BF16, name="held", tag="held", align_bytes=64)
-        quantise_pairs(last, 0, held)
+            second_stage(first_half[nt], 0, 0, nt)
+
+        second_half = {nt: sum_bank(FIRST_STAGE_BANKS[nt - REUSED_BANKS]) for nt in range(REUSED_BANKS, N_TILES)}
         for t in range(PACK):
-            tabs = keep.tile([P, HALF], F32, name="after", tag="held", align_bytes=64) if t == HT else None
-            pick(last, t, HALF, PAIRS, tabs)
+            pick(LAST, t, 0, HALF, tab_tile(HALF))
+            if t % 2 == 0:
+                quantise_pairs(LAST - 1, t // 2, woven_tile())
         for nt in range(N_TILES):
-            second_stage(early[nt], last, 0, nt)
+            second_stage(first_half[nt], LAST - 1, 0, nt)
+        for nt in range(REUSED_BANKS, N_TILES):
+            for b in range(LAST):
+                second_stage(second_half[nt], b, 1, nt)
+        held_woven = keep.tile([P, 2, HALF * PACK], BF16, tag="held", align_bytes=64)
+        quantise_pairs(LAST, 0, held_woven)
+        for t in range(PACK):
+            if t == HELD_SLICE:
+                tabs = keep.tile([P, HALF], F32, name="held_tabs", tag="held", align_bytes=64)
+            else:
+                tabs = tab_tile(HALF)
+            pick(LAST, t, HALF, PAIRS, tabs)
+        for nt in range(N_TILES):
+            second_stage(first_half[nt], LAST, 0, nt)
 
-        def turn_over(nt):
-            store(early[nt], 0, nt)
-            if nt < REUSED:
-                late[nt] = sum_bank(nt)
-                for b in range(last):
-                    second_stage(late[nt], b, 1, nt)
+        def finish_first_half(nt):
+            store(first_half[nt], 0, nt)
+            if nt < REUSED_BANKS:
+                second_half[nt] = sum_bank(nt)
+                for b in range(LAST):
+                    second_stage(second_half[nt], b, 1, nt)
 
-        for nt in range(EARLY):
-            turn_over(nt)
-        quantise_pairs(last, 1, None, nc.vector.tensor_copy)
-        for nt in range(EARLY, N_TILES):
-            turn_over(nt)
+        for nt in range(EMPTIED_EARLY):
+            finish_first_half(nt)
+        quantise_last_pairs()
+        for nt in range(EMPTIED_EARLY, N_TILES):
+            finish_first_half(nt)
         for nt in reversed(range(N_TILES)):
-            second_stage(late[nt], last, 1, nt)
-            store(late[nt], 1, nt)
+            second_stage(second_half[nt], LAST, 1, nt)
+            store(second_half[nt], 1, nt)

from contextlib import ExitStack

import concourse.mybir as mybir

K, T, S, PAIRS, H, N = 1024, 4096, 1024, 512, 1536, 640
FLOPS = 2 * K * H * S + 2 * 2 * H * N * PAIRS

F32 = mybir.dt.float32
BF16 = mybir.dt.bfloat16
I32 = mybir.dt.int32
U32 = mybir.dt.uint32
U16 = mybir.dt.uint16
U8 = mybir.dt.uint8
FP8X4 = mybir.dt.float8_e4m3fn_x4
FP4X4 = mybir.dt.float4_e2m1fn_x4
ALU = mybir.AluOpType
ACT = mybir.ActivationFunctionType

P = 128
PACK = 4
K_PASS = P * PACK
K_PASSES = K // K_PASS
H_PASSES = H // K_PASS
LAST = H_PASSES - 1
QUADRANTS = 4
BANK = 512
HALF = PAIRS // 2
N_TILES = N // P
FIRST_STAGE_BANKS = (5, 6, 7)
SCALE_ROW0 = P - 16 * K_PASSES
SYNC_MOVES = 6
AHEAD = 2
HELD_SLICE = 2
REUSED_BANKS = 3
EMPTIED_EARLY = 2


def tile_list_jigsaw_edge_fit_kernel(
    tc, tab_words, tab_scales, offs, pos1, pos2, w1, b1, gain, w2_words, w2_scales, out
):
    nc = tc.nc
    with ExitStack() as ctx:
        keep = ctx.enter_context(tc.tile_pool(name="keep", bufs=1))
        ring = ctx.enter_context(tc.tile_pool(name="ring", bufs=2))
        tab_ring = ctx.enter_context(tc.tile_pool(name="tab_ring", bufs=3))
        result_ring = ctx.enter_context(tc.tile_pool(name="result_ring", bufs=8))
        psum = ctx.enter_context(tc.psum_pool(name="psum", bufs=1))

        offs_t = keep.tile([P, S // 16], U16)
        pos1_t = keep.tile([P, PAIRS // 16], U16)
        pos2_t = keep.tile([P, PAIRS // 16], U16)
        table = [keep.tile([P, T], U16, name=f"table{a}", tag=f"stage{2 * a}", align_bytes=64) for a in range(K_PASSES)]
        table_scales = keep.tile([P, T], U8, align_bytes=64)
        v_words = [keep.tile([P, S], U16, name=f"v_words{a}", align_bytes=64) for a in range(K_PASSES)]
        picked_scales = keep.tile([P, S], U8, tag="picked", align_bytes=64)
        v_scales = [keep.tile([P, S], U8, name=f"v_scales{a}", align_bytes=64) for a in range(K_PASSES)]
        bias_t = keep.tile([P, H_PASSES, PACK], F32)
        gain_t = keep.tile([P, H_PASSES, PACK], F32)

        w1_mx = {}
        h_slices = {}
        planes = {}
        pair_mx = {}

        def load_w1(b, a, stage):
            raw = keep.tile([P, PACK, K_PASS], F32, name=f"raw{b}{a}", tag=f"stage{stage}", align_bytes=64)
            src = w1[a * K_PASS : (a + 1) * K_PASS, b * K_PASS : (b + 1) * K_PASS]
            nc.sync.dma_start(raw[:], src.rearrange("(p j) c -> p j c", j=PACK))
            return raw

        def quantise_w1(b, a, raw, casts, grouped):
            codes = keep.tile([P, K_PASS], U32, name=f"w1_codes{b}{a}", align_bytes=64)
            scales = keep.tile([P, K_PASS], U8, name=f"w1_scales{b}{a}", align_bytes=64)
            share = PACK // len(casts)
            for part, cast in enumerate(casts):
                ts = slice(part * share, (part + 1) * share)
                us = slice(ts.start // 2, ts.stop // 2)
                cols = slice(ts.start * P, ts.stop * P)
                cast(
                    grouped[:, ts, :].rearrange("p (u e) (m j) -> p u m j e", e=2, j=PACK),
                    raw[:].rearrange("p j (m u e) -> p u m j e", u=2, e=2)[:, us],
                )
                nc.vector.quantize_mx(
                    out=codes[:, cols].bitcast(FP8X4),
                    scales=scales[:, cols],
                    in_=grouped[:, ts, :].rearrange("p t c -> p (t c)"),
                )
            w1_mx[b, a] = codes, scales

        def grouped_tile():
            return ring.tile([P, PACK, P * PACK], BF16, name="grouped", align_bytes=64)

        def first_stage(b, t):
            s = b * PACK + t
            tag = f"stage{s - 1}" if AHEAD <= s <= PACK else f"row{s}"
            h = keep.tile([P, S], F32, name=f"h{s}", tag=tag, align_bytes=64)
            cols = slice(t * P, (t + 1) * P)
            for u in range(S // BANK):
                turn = s * (S // BANK) + u
                bank = FIRST_STAGE_BANKS[turn % len(FIRST_STAGE_BANKS)]
                acc = psum.tile([P, BANK], F32, name="acc", tag=f"bank{bank}")
                picked = slice(u * BANK, (u + 1) * BANK)
                for a in range(K_PASSES):
                    codes, scales = w1_mx[b, a]
                    nc.tensor.matmul_mx(
                        out=acc[:],
                        lhsT=codes[:, cols].bitcast(FP8X4),
                        lhsT_scale=scales[:, cols],
                        rhs=v_words[a][:, picked].bitcast(FP4X4),
                        rhs_scale=v_scales[a][:, picked],
                        start=(a == 0),
                        stop=(a == K_PASSES - 1),
                    )
                nc.scalar.activation(h[:, picked], acc[:], ACT.Tanh, bias=bias_t[:, b, t : t + 1])
            h_slices[b, t] = h

        def tab_tile(width):
            return tab_ring.tile([P, width], F32, name="tabs")

        def pick(b, t, m0, m1, tabs):
            h = h_slices[b, t]
            both, gap = planes[b]
            cols = slice(m0, m1)
            entries = slice(m0 // 16, m1 // 16)
            nc.vector.tensor_copy(tabs[:], h[:].indirect(pos1_t[:, entries]))
            pair_sum = ring.tile([P, m1 - m0], F32, name="pair_sum")
            nc.vector.tensor_tensor(pair_sum[:], h[:].indirect(pos2_t[:, entries]), tabs[:], ALU.add)
            nc.scalar.activation(both[:, t, cols], pair_sum[:], ACT.Copy, scale=gain_t[:, b, t : t + 1])
            nc.vector.scalar_tensor_tensor(
                gap[:, t, cols], tabs[:], gain2_t[:, b, t : t + 1], both[:, t, cols], ALU.mult, ALU.subtract
            )

        def woven_views(b, half, woven):
            cols = slice(half * HALF, (half + 1) * HALF)
            return [
                (
                    woven[:, kind, :].rearrange("p (c i t) -> p c t i", i=2, t=PACK),
                    plane[:, :, cols].rearrange("p t (c i) -> p c t i", i=2),
                )
                for kind, plane in enumerate(planes[b])
            ]

        def pair_tiles(b, half):
            codes = keep.tile([P, BANK], U32, name=f"pair_codes{b}{half}", align_bytes=64)
            scales = keep.tile([P, BANK], U8, name=f"pair_scales{b}{half}", align_bytes=64)
            pair_mx[b, half] = codes, scales
            return codes, scales

        def woven_tile():
            return ring.tile([P, 2, HALF * PACK], BF16, name="woven", align_bytes=64)

        def quantise_pairs(b, half, woven):
            (both_dst, both_src), (gap_dst, gap_src) = woven_views(b, half, woven)
            nc.scalar.activation(both_dst, both_src, ACT.Copy)
            nc.scalar.activation(gap_dst, gap_src, ACT.Abs)
            codes, scales = pair_tiles(b, half)
            nc.vector.quantize_mx(
                out=codes[:].bitcast(FP8X4), scales=scales[:], in_=woven[:].rearrange("p k c -> p (k c)")
            )

        def quantise_last_pairs():
            woven = woven_tile()
            (both_dst, both_src), (gap_dst, gap_src) = woven_views(LAST, 1, woven)
            nc.vector.tensor_copy(both_dst, both_src)
            nc.scalar.activation(gap_dst, gap_src, ACT.Abs)
            codes, scales = pair_tiles(LAST, 1)
            for kind in range(2):
                part = slice(kind * HALF, (kind + 1) * HALF)
                nc.vector.quantize_mx(out=codes[:, part].bitcast(FP8X4), scales=scales[:, part], in_=woven[:, kind, :])

        def sum_bank(bank):
            return psum.tile([P, BANK], F32, name="y", tag=f"bank{bank}")

        def second_stage(y, b, half, nt):
            codes, scales = pair_mx[b, half]
            nc.tensor.matmul_mx(
                out=y[:],
                lhsT=w2_t[:, b, 2 * P * nt : 2 * P * (nt + 1)].bitcast(FP4X4),
                lhsT_scale=w2_s[:, b, P * nt : P * (nt + 1)],
                rhs=codes[:].bitcast(FP8X4),
                rhs_scale=scales[:],
                start=(b == 0),
                stop=(b == LAST),
            )

        def store(y, half, nt):
            y1 = result_ring.tile([P, HALF], F32, name="y1")
            nc.scalar.copy(y1[:], y[:, :HALF])
            fit = result_ring.tile([P, HALF], F32, name="fit")
            nc.vector.tensor_tensor(fit[:], y[:, HALF:], y1[:], ALU.min)
            nc.sync.dma_start(out[nt * P : (nt + 1) * P, half * HALF : (half + 1) * HALF], fit[:])

        nc.sync.dma_start(offs_t[:], offs)
        nc.sync.dma_start(
            table_scales[SCALE_ROW0:P, :].bitcast(I32), tab_scales.rearrange("a q t -> (a q) t").bitcast(I32)
        )
        nc.vector.memset(table_scales[0:SCALE_ROW0, :].bitcast(I32), 0)
        for a in range(K_PASSES):
            nc.vector.memset(v_scales[a][:].bitcast(I32), 0)
        nc.sync.dma_start(pos1_t[:], pos1)
        nc.sync.dma_start(pos2_t[:], pos2)
        nc.sync.dma_start(table[0][:].bitcast(I32), tab_words[0].bitcast(I32))
        raw_first = load_w1(0, 0, 1)
        nc.sync.dma_start(table[1][:].bitcast(I32), tab_words[1].bitcast(I32))
        raw_second = load_w1(0, 1, 3)
        nc.gpsimd.dma_start(bias_t[:], b1.rearrange("(b p t) -> p b t", p=P, t=PACK))
        nc.gpsimd.dma_start(gain_t[:], gain.rearrange("(b p t) -> p b t", p=P, t=PACK))

        nc.vector.tensor_copy(picked_scales[:], table_scales[:].indirect(offs_t[:]))
        for a in range(K_PASSES):
            for q in range(QUADRANTS):
                row = SCALE_ROW0 + 16 * a + 4 * q
                queue = nc.sync if QUADRANTS * a + q < SYNC_MOVES else nc.gpsimd
                queue.dma_start(
                    v_scales[a][32 * q : 32 * q + 4, :].bitcast(I32), picked_scales[row : row + 4, :].bitcast(I32)
                )
        gain2_t = keep.tile([P, H_PASSES, PACK], F32, tag="picked", align_bytes=64)
        nc.gpsimd.tensor_scalar(gain2_t[:], gain_t[:], 2.0, 0.0, ALU.mult, ALU.add)
        shared_cast = [nc.vector.tensor_copy, nc.scalar.copy]
        nc.vector.tensor_copy(v_words[0][:], table[0][:].indirect(offs_t[:]))
        quantise_w1(0, 0, raw_first, shared_cast, grouped_tile())
        nc.vector.tensor_copy(v_words[1][:], table[1][:].indirect(offs_t[:]))
        quantise_w1(0, 1, raw_second, shared_cast, grouped_tile())

        for b in range(H_PASSES):
            planes[b] = (
                keep.tile([P, PACK, PAIRS], F32, name=f"both{b}"),
                keep.tile([P, PACK, PAIRS], F32, name=f"gap{b}"),
            )
        first_half = [sum_bank(nt) for nt in range(N_TILES)]
        for t in range(AHEAD):
            first_stage(0, t)

        early_grouped = keep.tile([P, PACK, P * PACK], BF16, tag="early", align_bytes=64)
        quantise_w1(1, 0, load_w1(1, 0, 0), [nc.vector.tensor_copy], early_grouped)
        taken_over = ("stage0", "early")
        for t in range(PACK):
            if t < len(taken_over):
                tabs = keep.tile([P, PAIRS], F32, name="first_tabs", tag=taken_over[t], align_bytes=64)
            else:
                tabs = tab_tile(PAIRS)
            pick(0, t, 0, PAIRS, tabs)
            if t + 1 < PACK:
                b, a = divmod(K_PASSES + t + 1, K_PASSES)
                quantise_w1(b, a, load_w1(b, a, t + 1), [nc.scalar.copy], grouped_tile())
            first_stage(*divmod(t + AHEAD, PACK))

        w2_t = keep.tile([P, H_PASSES, 2 * N], U8, tag="row0", align_bytes=64)
        w2_s = keep.tile([P, H_PASSES, N], U8, tag="row1", align_bytes=64)
        nc.sync.dma_start(w2_t[:].bitcast(I32), w2_words.rearrange("a p c -> p a c").bitcast(I32))
        nc.gpsimd.memset(w2_s[:].bitcast(I32), 0)
        for q in range(QUADRANTS):
            nc.sync.dma_start(
                w2_s[32 * q : 32 * q + 4].bitcast(I32),
                w2_scales[:, 4 * q : 4 * q + 4, :].rearrange("a r n -> r a n").bitcast(I32),
            )

        next_slice = PACK + AHEAD
        for t in range(PACK):
            pick(1, t, 0, PAIRS, tab_tile(PAIRS))
            if t % 2 == 0:
                quantise_pairs(0, t // 2, woven_tile())
            made = 1 if t % 2 == 0 else 2
            for s in range(next_slice, next_slice + made):
                first_stage(*divmod(s, PACK))
            next_slice = next_slice + made
        for nt in range(N_TILES):
            second_stage(first_half[nt], 0, 0, nt)

        second_half = {nt: sum_bank(FIRST_STAGE_BANKS[nt - REUSED_BANKS]) for nt in range(REUSED_BANKS, N_TILES)}
        for t in range(PACK):
            pick(LAST, t, 0, HALF, tab_tile(HALF))
            if t % 2 == 0:
                quantise_pairs(LAST - 1, t // 2, woven_tile())
        for nt in range(N_TILES):
            second_stage(first_half[nt], LAST - 1, 0, nt)
        for nt in range(REUSED_BANKS, N_TILES):
            for b in range(LAST):
                second_stage(second_half[nt], b, 1, nt)
        held_woven = keep.tile([P, 2, HALF * PACK], BF16, tag="held", align_bytes=64)
        quantise_pairs(LAST, 0, held_woven)
        for t in range(PACK):
            if t == HELD_SLICE:
                tabs = keep.tile([P, HALF], F32, name="held_tabs", tag="held", align_bytes=64)
            else:
                tabs = tab_tile(HALF)
            pick(LAST, t, HALF, PAIRS, tabs)
        for nt in range(N_TILES):
            second_stage(first_half[nt], LAST, 0, nt)

        def finish_first_half(nt):
            store(first_half[nt], 0, nt)
            if nt < REUSED_BANKS:
                second_half[nt] = sum_bank(nt)
                for b in range(LAST):
                    second_stage(second_half[nt], b, 1, nt)

        for nt in range(EMPTIED_EARLY):
            finish_first_half(nt)
        quantise_last_pairs()
        for nt in range(EMPTIED_EARLY, N_TILES):
            finish_first_half(nt)
        for nt in reversed(range(N_TILES)):
            second_stage(second_half[nt], LAST, 1, nt)
            store(second_half[nt], 1, nt)
